import numpy as np
import ml_dtypes


def mxq(x, axis, fmt="e4m3"):
    dtype, down = {"e4m3": (ml_dtypes.float8_e4m3fn, 7), "e5m2": (ml_dtypes.float8_e5m2, 14)}[fmt]
    v = np.moveaxis(np.asarray(x, np.float32).astype(ml_dtypes.bfloat16).astype(np.float64), axis, -1)
    blocks = v.reshape(v.shape[:-1] + (-1, 32))
    amax = np.abs(blocks).max(-1, keepdims=True)
    byte = np.maximum(np.where(amax > 0, np.frexp(amax)[1] - 1 + 127, 0) - down, 1)
    scale = np.exp2(byte - 127.0)
    codes = (blocks / scale).astype(np.float32).astype(dtype).astype(np.float64)
    return np.moveaxis((codes * scale).reshape(v.shape), -1, axis)


WIDE = False


def mx_kscale(k):
    if not WIDE:
        return np.ones(k)
    levels = np.array([10, -10, 5, -5, 0])
    if k % 512:
        return np.exp2(np.random.permutation(np.resize(levels, k // 32))).repeat(32)
    a = np.empty((k // 512, 16))
    for p in range(k // 512):
        a[p, :8] = np.random.permutation(np.resize(levels, 8))
        for g in range(8):
            far = levels[np.abs(levels - a[p, g]) >= 10]
            a[p, g + 8] = far[np.random.randint(len(far))]
    return np.exp2(a.ravel()).repeat(32)


def f64(x):
    return np.asarray(x).astype(np.float64)


def striped(idx):
    return np.tile(idx.reshape(-1, 16).T, (8, 1)).astype(np.uint16)


def unstriped(offs):
    return offs[:16].T.reshape(-1).astype(np.int64)


def pack_weight(w):
    k, n = w.shape
    w = f64(np.asarray(w, np.float32).astype(ml_dtypes.bfloat16)).reshape(k // 32, 32, n)
    amax = np.abs(w).max(1)
    byte = np.clip(np.where(amax > 0, np.frexp(amax)[1] - 1 + 127 - 7, 1), 1, 254)
    scaled = (w * np.exp2(127.0 - byte)[:, None, :]).reshape(k, n).astype(np.float32)
    words = np.ascontiguousarray(scaled.reshape(k // 512, 128, 4, n).transpose(0, 1, 3, 2)).astype(ml_dtypes.float8_e4m3fn).view(np.uint8)
    return words, np.ascontiguousarray(byte.astype(np.uint8).reshape(k // 512, 16, n))


def unpack_weight(words, scales):
    g, p, n, _ = words.shape
    vals = np.ascontiguousarray(words).view(ml_dtypes.float8_e4m3fn).astype(np.float64) * np.repeat(np.exp2(scales.astype(np.float64) - 127.0), 8, axis=1)[..., None]
    return vals.transpose(0, 1, 3, 2).reshape(g * 512, n)


E2M1 = np.array([0.0, 0.5, 1.0, 1.5, 2.0, 3.0, 4.0, 6.0, -0.0, -0.5, -1.0, -1.5, -2.0, -3.0, -4.0, -6.0])


def pack_fp4(w):
    k, n = w.shape
    w = f64(np.asarray(w, np.float32).astype(ml_dtypes.bfloat16)).reshape(k // 32, 32, n)
    amax = np.abs(w).max(1)
    mant, ex = np.frexp(amax / 6.0)
    byte = np.clip(np.where(amax > 0, np.where(mant > 0.5, ex, ex - 1) + 127, 1), 1, 254)
    scaled = (w * np.exp2(127.0 - byte)[:, None, :]).reshape(k, n).astype(np.float32)
    c = np.ascontiguousarray(scaled.reshape(k // 512, 128, 4, n).transpose(0, 1, 3, 2)).astype(ml_dtypes.float4_e2m1fn).view(np.uint8) & 0xF
    words = (c[..., 0::2] | (c[..., 1::2] << 4)).reshape(k // 512, 128, 2 * n)
    return np.ascontiguousarray(words), np.ascontiguousarray(byte.astype(np.uint8).reshape(k // 512, 16, n))


def unpack_fp4(words, scales):
    g, _, n = scales.shape
    words = np.ascontiguousarray(words).reshape(g, 128, n, 2)
    nib = np.empty((g, 128, n, 4), np.uint8)
    nib[..., 0::2] = words & 0xF
    nib[..., 1::2] = words >> 4
    vals = E2M1[nib] * np.repeat(np.exp2(scales.astype(np.float64) - 127.0), 8, axis=1)[..., None]
    return vals.transpose(0, 1, 3, 2).reshape(g * 512, n)


def sigmoid(v):
    return 1.0 / (1.0 + np.exp(-np.maximum(v, -700.0)))


K, T, S, N, H = 1024, 2048, 512, 256, 512


def setup_inputs():
    n = np.random.standard_normal
    s = mx_kscale(K)[:, None]
    u = mx_kscale(H)
    packed_xT = pack_weight(n((K, T)) * s)
    packed_w1 = pack_fp4(n((K, H)) / np.sqrt(K) / s)
    packed_w2 = pack_fp4(n((K, H)) / np.sqrt(K) / s)
    packed_w3 = pack_fp4(n((H, N)) / np.sqrt(H) / u[:, None])
    return {
        "x_words": packed_xT[0],
        "x_scales": packed_xT[1],
        "w1_words": packed_w1[0],
        "w1_scales": packed_w1[1],
        "w2_words": packed_w2[0],
        "w2_scales": packed_w2[1],
        "dust": (np.random.uniform(0.1, 0.5, (H, S))).astype(np.float32),
        "unit": (np.random.uniform(0.6, 1.4, (H, 1)) * u[:, None]).astype(np.float32),
        "w3_words": packed_w3[0],
        "w3_scales": packed_w3[1],
        "offs": striped(np.random.permutation(T)[:S]),
        "src": striped(np.random.permutation(S)),
    }


def reference(x_words, x_scales, w1_words, w1_scales, w2_words, w2_scales, dust, unit, w3_words, w3_scales, offs, src):
    xq = unpack_weight(x_words, x_scales)[:, unstriped(offs)]
    ts = unpack_fp4(w1_words, w1_scales).T @ xq
    melt = sigmoid(2.0 * ts)
    ag = unpack_fp4(w2_words, w2_scales).T @ xq
    age = np.log(np.exp(ag) + 1.0)
    cold = (-1.0 * melt + 1.0) * np.exp(-1.0 * age)
    wet = melt * np.exp(-1.8 * age)
    as_ = age[:, unstriped(src)]
    dst = as_ * f64(dust)
    alb = (cold + wet + 0.2) / (dst + 1.0)
    hid = f64(unit) * ((-1.0 * alb + 1.0) * (np.log(np.exp(ts[:, unstriped(src)]) + 1.0)))
    return unpack_fp4(w3_words, w3_scales).T @ mxq(hid, 0, "e4m3")

@@ -1,0 +1,231 @@
+from contextlib import ExitStack
+
+import concourse.mybir as mybir
+
+K, T, S, N, H = 1024, 2048, 512, 256, 512
+FLOPS = 2 * (2 * K * H * S + H * N * S)
+
+F32 = mybir.dt.float32
+BF16 = mybir.dt.bfloat16
+I32 = mybir.dt.int32
+U32 = mybir.dt.uint32
+U16 = mybir.dt.uint16
+U8 = mybir.dt.uint8
+FP8X4 = mybir.dt.float8_e4m3fn_x4
+FP4X4 = mybir.dt.float4_e2m1fn_x4
+ACT = mybir.ActivationFunctionType
+ALU = mybir.AluOpType
+
+P = 128
+PACK = 4
+PASSES = K // (P * PACK)
+QUADS = 4
+TS_SPARE = 192
+AGE_SPARE = 32
+CHUNK = 128
+TINY = 2.0 ** -62
+
+
+def load_scale_rows(queue, tile, rows, passes):
+    for q in range(QUADS):
+        queue.dma_start(
+            out=tile[32 * q : 32 * q + 4, :].bitcast(I32).rearrange("p (o c) -> p o c", o=passes),
+            in_=rows[:, 4 * q : 4 * q + 4, :].bitcast(I32).rearrange("o r c -> r o c"),
+        )
+
+
+def tile_picked_ysnowa_abs_p_kernel(
+    tc, x_words, x_scales, w1_words, w1_scales, w2_words, w2_scales, dust, unit, w3_words, w3_scales, offs, src, out
+):
+    nc = tc.nc
+    with ExitStack() as ctx:
+        lists = ctx.enter_context(tc.tile_pool(name="lists", bufs=1))
+        sb = ctx.enter_context(tc.tile_pool(name="sb", bufs=1))
+        psum = ctx.enter_context(tc.psum_pool(name="psum", bufs=1))
+
+        offs_sb = lists.tile([P, S // 16], U16, name="offs_sb")
+        src_sb = lists.tile([P, S // 16], U16, name="src_sb")
+        nc.sync.dma_start(offs_sb[:], offs)
+
+        x_scale_rows = sb.tile([P, PASSES * T], U8, name="x_scale_rows", tag="x_scale_rows", align_bytes=64)
+        nc.vector.memset(x_scale_rows[:].bitcast(I32), 0)
+        w_raw = []
+        w_scale_raw = []
+        for i, words in enumerate((w1_words, w2_words)):
+            raw = sb.tile([P, PASSES * 2 * H], U8, name="w_raw%d" % i, tag="w_raw%d" % i, align_bytes=64)
+            nc.sync.dma_start(
+                out=raw[:].bitcast(I32).rearrange("p (o c) -> p o c", o=PASSES),
+                in_=words.bitcast(I32).rearrange("o p c -> p o c"),
+            )
+            w_raw.append(raw)
+            scale_raw = sb.tile([P, PASSES * H], U8, name="w_scale_raw%d" % i, tag="w_scale_raw%d" % i, align_bytes=64)
+            w_scale_raw.append(scale_raw)
+        nc.gpsimd.memset(w_scale_raw[0][:].bitcast(I32), 0)
+        nc.vector.memset(w_scale_raw[1][:].bitcast(I32), 0)
+        load_scale_rows(nc.gpsimd, w_scale_raw[0], w1_scales, PASSES)
+        load_scale_rows(nc.sync, x_scale_rows, x_scales, PASSES)
+        x_word_rows = []
+        for o in range(PASSES):
+            rows = sb.tile([P, T], U32, name="x_word_rows%d" % o, tag="x_word_rows%d" % o)
+            nc.sync.dma_start(out=rows[:].bitcast(I32), in_=x_words[o].rearrange("p c r -> p (c r)").bitcast(I32))
+            x_word_rows.append(rows)
+        load_scale_rows(nc.sync, w_scale_raw[1], w2_scales, PASSES)
+        nc.sync.dma_start(src_sb[:], src)
+
+        w_codes = []
+        for i in range(2):
+            codes = sb.tile([P, PASSES * 2 * H], U8, name="w_codes%d" % i, align_bytes=64)
+            nc.vector.tensor_copy(
+                out=codes[:].bitcast(U16).rearrange("p (o t m) -> p o t m", o=PASSES, t=PACK),
+                in_=w_raw[i][:].bitcast(U16).rearrange("p (o m t) -> p o t m", o=PASSES, t=PACK),
+            )
+            w_codes.append(codes)
+        x_picked_scales = []
+        for o in range(PASSES):
+            picked = sb.tile([P, S], U8, name="x_picked_scales%d" % o, align_bytes=64)
+            nc.vector.tensor_copy(picked[:], x_scale_rows[:, o * T : (o + 1) * T].indirect(offs_sb[:]))
+            x_picked_scales.append(picked)
+
+        def deal_scales(i, tag):
+            scales = sb.tile([P, PASSES * H], U8, name="w_scales%d" % i, tag=tag, align_bytes=64)
+            nc.vector.tensor_copy(
+                out=scales[:].rearrange("p (o t m) -> p o t m", o=PASSES, t=PACK),
+                in_=w_scale_raw[i][:].rearrange("p (o m t) -> p o t m", o=PASSES, t=PACK),
+            )
+            return scales
+
+        def pick_words(o, tag):
+            codes = sb.tile([P, S], U32, name="x_codes%d" % o, tag=tag, align_bytes=64)
+            nc.vector.tensor_copy(codes[:], x_word_rows[o][:].indirect(offs_sb[:]))
+            return codes
+
+        x_codes = [pick_words(0, "x_codes0")]
+        w_scales = [deal_scales(0, "x_scale_rows")]
+        x_codes.append(pick_words(1, "w_scale_raw0"))
+        w_scales.append(deal_scales(1, "w_scales1"))
+
+        dust_sb = sb.tile([P, PACK, S], F32, name="dust_sb", tag="x_word_rows0")
+        nc.sync.dma_start(out=dust_sb[:], in_=dust.rearrange("(p t) j -> p t j", t=PACK))
+        w3_codes = sb.tile([P, 2 * N], U8, name="w3_codes", tag="w_raw0", align_bytes=64)
+        nc.sync.dma_start(out=w3_codes[:].bitcast(I32), in_=w3_words[0].bitcast(I32))
+        unit_sb = sb.tile([P, PACK], F32, name="unit_sb", tag="w_raw1", align_bytes=64)
+        nc.sync.dma_start(out=unit_sb[:], in_=unit.rearrange("(p t) one -> p (t one)", t=PACK))
+        w3_scale_rows = sb.tile([P, N], U8, name="w3_scale_rows", tag="w_scale_raw1", align_bytes=64)
+        nc.gpsimd.memset(w3_scale_rows[:].bitcast(I32), 0)
+        load_scale_rows(nc.sync, w3_scale_rows, w3_scales, 1)
+
+        def product(i, t):
+            bank = psum.tile([P, S], F32, name="bank%d_%d" % (i, t), tag="bank%d" % (PACK * i + t))
+            for o in range(PASSES):
+                col = (o * PACK + t) * P
+                nc.tensor.matmul_mx(
+                    out=bank[:],
+                    lhsT=w_codes[i][:, 2 * col : 2 * (col + P)].bitcast(FP4X4),
+                    lhsT_scale=w_scales[i][:, col : col + P],
+                    rhs=x_codes[o][:].bitcast(FP8X4),
+                    rhs_scale=x_picked_scales[o][:],
+                    start=(o == 0),
+                    stop=(o == PASSES - 1),
+                )
+            return bank
+
+        ts = [product(0, t) for t in range(PACK)]
+        ag = [product(1, t) for t in range(PACK)]
+
+        neg_ts = sb.tile([P, PACK * S + TS_SPARE], F32, name="neg_ts", tag="before_ln")
+        nc.vector.memset(neg_ts[:, PACK * S :], 0.0)
+        neg_ts_src = sb.tile([P, PACK, S], F32, name="neg_ts_src")
+        melt = sb.tile([P, PACK, S], F32, name="melt")
+        fresh = sb.tile([P, PACK, S], F32, name="fresh")
+        sig_src = sb.tile([P, PACK, S], F32, name="sig_src")
+        for t in range(PACK):
+            lo = (PACK - 1 - t) * S
+            nc.vector.tensor_scalar(neg_ts[:, lo : lo + S], ts[t][:], -1.0, None, ALU.mult)
+            nc.vector.tensor_copy(neg_ts_src[:, t, :], neg_ts[:, lo : lo + S + TS_SPARE].indirect(src_sb[:]))
+        for t in range(PACK):
+            lo = (PACK - 1 - t) * S
+            nc.scalar.activation(melt[:, t, :], neg_ts[:, lo : lo + S], ACT.Sigmoid, scale=-2.0)
+            nc.scalar.activation(fresh[:, t, :], ag[t][:], ACT.Sigmoid, scale=-1.0)
+        for t in range(PACK):
+            nc.scalar.activation(sig_src[:, t, :], neg_ts_src[:, t, :], ACT.Sigmoid)
+
+        logs = sb.tile([P, 2, PACK, S], F32, name="logs", tag="before_ln")
+        ln_fresh = logs[:, 0]
+        ln_sig = logs[:, 1]
+        dst = sb.tile([P, PACK, S], F32, name="dst")
+        ln_den = sb.tile([P, PACK, S], F32, name="ln_den")
+        for t in range(PACK):
+            nc.scalar.activation(ln_fresh[:, t, :], fresh[:, t, :], ACT.Ln, bias=TINY)
+        for t in range(PACK):
+            age = sb.tile([P, S + AGE_SPARE], F32, name="age%d" % t)
+            nc.vector.memset(age[:, S:], 0.0)
+            nc.vector.scalar_tensor_tensor(age[:, :S], ln_fresh[:, t, :], -1.0, ag[t][:], ALU.mult, ALU.max)
+            nc.vector.tensor_tensor(dst[:, t, :], age[:].indirect(src_sb[:]), dust_sb[:, t, :], ALU.mult)
+        for h in range(2):
+            nc.scalar.activation(ln_sig[:, 2 * h : 2 * h + 2, :], sig_src[:, 2 * h : 2 * h + 2, :], ACT.Ln, bias=TINY)
+        for t in range(PACK):
+            nc.scalar.activation(ln_den[:, t, :], dst[:, t, :], ACT.Ln, bias=1.0)
+
+        neg_soft = sb.tile([P, PACK, S], F32, name="neg_soft")
+        neg_gain = sb.tile([P, PACK, S], F32, name="neg_gain")
+        for h in range(2):
+            rows = slice(2 * h, 2 * h + 2)
+            nc.vector.tensor_tensor(neg_soft[:, rows, :], neg_ts_src[:, rows, :], ln_sig[:, rows, :], ALU.min)
+        for t in range(PACK):
+            nc.vector.tensor_scalar(neg_gain[:, t, :], neg_soft[:, t, :], unit_sb[:, t : t + 1], None, ALU.mult)
+
+        exps = sb.tile([P, 2, PACK, S], F32, name="exps", tag="x_word_rows0")
+        ratio = exps[:, 0]
+        inv_den = exps[:, 1]
+        halves = [slice(c, c + S // 2) for c in range(0, S, S // 2)]
+        chunks = [slice(c, c + CHUNK) for c in range(0, S, CHUNK)]
+        for cols in chunks:
+            nc.scalar.activation(ratio[:, :, cols], ln_fresh[:, :, cols], ACT.Exp, scale=0.8)
+        for cols in halves:
+            nc.scalar.activation(inv_den[:, :, cols], ln_den[:, :, cols], ACT.Exp, scale=-1.0)
+
+        mixed = sb.tile([P, PACK, S], F32, name="mixed")
+        dark = sb.tile([P, PACK, S], F32, name="dark")
+        alb = sb.tile([P, PACK, S], F32, name="alb")
+        hid = sb.tile([P, PACK, S], BF16, name="hid")
+
+        def finish(c):
+            cols = chunks[c]
+            woven = sb.tile([P, CHUNK, PACK], BF16, name="woven%d" % c, align_bytes=64)
+            weave = nc.vector.tensor_copy if c == len(chunks) - 1 else nc.scalar.copy
+            weave(
+                woven[:].rearrange("p (g i) t -> p g t i", i=4),
+                hid[:, :, cols].rearrange("p t (g i) -> p g t i", i=4),
+            )
+            hid_codes = sb.tile([P, CHUNK], U32, name="hid_codes%d" % c, align_bytes=64)
+            hid_scales = sb.tile([P, CHUNK], U8, name="hid_scales%d" % c, align_bytes=64)
+            nc.vector.quantize_mx(
+                out=hid_codes[:].bitcast(FP8X4), scales=hid_scales[:], in_=woven[:].rearrange("p j t -> p (j t)")
+            )
+            bands = psum.tile([P, N // P, CHUNK], F32, name="bands%d" % c, tag="bank%d" % c)
+            for m in range(N // P):
+                nc.tensor.matmul_mx(
+                    out=bands[:, m, :],
+                    lhsT=w3_codes[:, 2 * m * P : 2 * (m + 1) * P].bitcast(FP4X4),
+                    lhsT_scale=w3_scale_rows[:, m * P : (m + 1) * P],
+                    rhs=hid_codes[:].bitcast(FP8X4),
+                    rhs_scale=hid_scales[:],
+                    start=True,
+                    stop=True,
+                )
+            result = sb.tile([P, N // P, CHUNK], F32, name="result%d" % c)
+            nc.scalar.copy(result[:], bands[:])
+            nc.sync.dma_start(out=out[:, cols].rearrange("(m p) j -> p m j", p=P), in_=result[:])
+
+        for h in range(2):
+            pair = chunks[2 * h : 2 * h + 2]
+            for cols in pair:
+                nc.vector.scalar_tensor_tensor(mixed[:, :, cols], ratio[:, :, cols], -1.0, melt[:, :, cols], ALU.add, ALU.mult)
+            for cols in pair:
+                nc.vector.scalar_tensor_tensor(dark[:, :, cols], mixed[:, :, cols], 1.0, fresh[:, :, cols], ALU.add, ALU.mult)
+            for cols in pair:
+                nc.vector.scalar_tensor_tensor(alb[:, :, cols], dark[:, :, cols], 0.2, inv_den[:, :, cols], ALU.add, ALU.mult)
+            for cols in pair:
+                nc.vector.scalar_tensor_tensor(hid[:, :, cols], alb[:, :, cols], -1.0, neg_gain[:, :, cols], ALU.add, ALU.mult)
+            for c in range(2 * h, 2 * h + 2):
+                finish(c)

@@ -26,14 +26,6 @@ CHUNK = 128
 TINY = 2.0 ** -62
 
 
-def load_scale_rows(queue, tile, rows, passes):
-    for q in range(QUADS):
-        queue.dma_start(
-            out=tile[32 * q : 32 * q + 4, :].bitcast(I32).rearrange("p (o c) -> p o c", o=passes),
-            in_=rows[:, 4 * q : 4 * q + 4, :].bitcast(I32).rearrange("o r c -> r o c"),
-        )
-
-
 def tile_picked_ysnowa_abs_p_kernel(
     tc, x_words, x_scales, w1_words, w1_scales, w2_words, w2_scales, dust, unit, w3_words, w3_scales, offs, src, out
 ):
@@ -47,39 +39,55 @@ def tile_picked_ysnowa_abs_p_kernel(
         src_sb = lists.tile([P, S // 16], U16, name="src_sb")
         nc.sync.dma_start(offs_sb[:], offs)
 
+        def load_scale_rows(tile, rows, passes, quads):
+            for q in quads:
+                nc.sync.dma_start(
+                    out=tile[32 * q : 32 * q + 4, :].bitcast(I32).rearrange("p (o c) -> p o c", o=passes),
+                    in_=rows[:, 4 * q : 4 * q + 4, :].bitcast(I32).rearrange("o r c -> r o c"),
+                )
+
         x_scale_rows = sb.tile([P, PASSES * T], U8, name="x_scale_rows", tag="x_scale_rows", align_bytes=64)
-        nc.vector.memset(x_scale_rows[:].bitcast(I32), 0)
+        nc.vector.memset(x_scale_rows[:, :T].bitcast(I32), 0)
+        nc.gpsimd.memset(x_scale_rows[:, T:].bitcast(I32), 0)
         w_raw = []
         w_scale_raw = []
-        for i, words in enumerate((w1_words, w2_words)):
-            raw = sb.tile([P, PASSES * 2 * H], U8, name="w_raw%d" % i, tag="w_raw%d" % i, align_bytes=64)
+        for i in range(2):
+            w_raw.append(sb.tile([P, PASSES * 2 * H], U8, name="w_raw%d" % i, tag="w_raw%d" % i, align_bytes=64))
+            scale_raw = sb.tile([P, PASSES * H], U8, name="w_scale_raw%d" % i, tag="w_scale_raw%d" % i, align_bytes=64)
+            nc.vector.memset(scale_raw[:].bitcast(I32), 0)
+            w_scale_raw.append(scale_raw)
+        x_word_rows = [sb.tile([P, T], U32, name="x_word_rows%d" % o, tag="x_word_rows%d" % o) for o in range(PASSES)]
+
+        def load_w_words(i, words):
             nc.sync.dma_start(
-                out=raw[:].bitcast(I32).rearrange("p (o c) -> p o c", o=PASSES),
+                out=w_raw[i][:].bitcast(I32).rearrange("p (o c) -> p o c", o=PASSES),
                 in_=words.bitcast(I32).rearrange("o p c -> p o c"),
             )
-            w_raw.append(raw)
-            scale_raw = sb.tile([P, PASSES * H], U8, name="w_scale_raw%d" % i, tag="w_scale_raw%d" % i, align_bytes=64)
-            w_scale_raw.append(scale_raw)
-        nc.gpsimd.memset(w_scale_raw[0][:].bitcast(I32), 0)
-        nc.vector.memset(w_scale_raw[1][:].bitcast(I32), 0)
-        load_scale_rows(nc.gpsimd, w_scale_raw[0], w1_scales, PASSES)
-        load_scale_rows(nc.sync, x_scale_rows, x_scales, PASSES)
-        x_word_rows = []
-        for o in range(PASSES):
-            rows = sb.tile([P, T], U32, name="x_word_rows%d" % o, tag="x_word_rows%d" % o)
-            nc.sync.dma_start(out=rows[:].bitcast(I32), in_=x_words[o].rearrange("p c r -> p (c r)").bitcast(I32))
-            x_word_rows.append(rows)
-        load_scale_rows(nc.sync, w_scale_raw[1], w2_scales, PASSES)
+
+        def load_x_words(o):
+            nc.sync.dma_start(
+                out=x_word_rows[o][:].bitcast(I32), in_=x_words[o].rearrange("p c r -> p (c r)").bitcast(I32)
+            )
+
+        load_w_words(0, w1_words)
+        load_scale_rows(x_scale_rows, x_scales, PASSES, range(QUADS))
+        load_scale_rows(w_scale_raw[0], w1_scales, PASSES, range(1))
+        load_x_words(0)
+        load_scale_rows(w_scale_raw[0], w1_scales, PASSES, range(1, QUADS))
+        load_x_words(1)
+        load_w_words(1, w2_words)
+        load_scale_rows(w_scale_raw[1], w2_scales, PASSES, range(QUADS))
         nc.sync.dma_start(src_sb[:], src)
 
-        w_codes = []
-        for i in range(2):
+        def deal_words(i):
             codes = sb.tile([P, PASSES * 2 * H], U8, name="w_codes%d" % i, align_bytes=64)
             nc.vector.tensor_copy(
-                out=codes[:].bitcast(U16).rearrange("p (o t m) -> p o t m", o=PASSES, t=PACK),
-                in_=w_raw[i][:].bitcast(U16).rearrange("p (o m t) -> p o t m", o=PASSES, t=PACK),
+                out=codes[:].bitcast(U16).rearrange("p (o t g m) -> p o g t m", o=PASSES, t=PACK, m=8),
+                in_=w_raw[i][:].bitcast(U16).rearrange("p (o g m t) -> p o g t m", o=PASSES, t=PACK, m=8),
             )
-            w_codes.append(codes)
+            return codes
+
+        w_codes = [deal_words(0)]
         x_picked_scales = []
         for o in range(PASSES):
             picked = sb.tile([P, S], U8, name="x_picked_scales%d" % o, align_bytes=64)
@@ -89,8 +97,8 @@ def tile_picked_ysnowa_abs_p_kernel(
         def deal_scales(i, tag):
             scales = sb.tile([P, PASSES * H], U8, name="w_scales%d" % i, tag=tag, align_bytes=64)
             nc.vector.tensor_copy(
-                out=scales[:].rearrange("p (o t m) -> p o t m", o=PASSES, t=PACK),
-                in_=w_scale_raw[i][:].rearrange("p (o m t) -> p o t m", o=PASSES, t=PACK),
+                out=scales[:].rearrange("p (o t g m) -> p o g t m", o=PASSES, t=PACK, m=16),
+                in_=w_scale_raw[i][:].rearrange("p (o g m t) -> p o g t m", o=PASSES, t=PACK, m=16),
             )
             return scales
 
@@ -102,6 +110,7 @@ def tile_picked_ysnowa_abs_p_kernel(
         x_codes = [pick_words(0, "x_codes0")]
         w_scales = [deal_scales(0, "x_scale_rows")]
         x_codes.append(pick_words(1, "w_scale_raw0"))
+        w_codes.append(deal_words(1))
         w_scales.append(deal_scales(1, "w_scales1"))
 
         dust_sb = sb.tile([P, PACK, S], F32, name="dust_sb", tag="x_word_rows0")
@@ -112,7 +121,7 @@ def tile_picked_ysnowa_abs_p_kernel(
         nc.sync.dma_start(out=unit_sb[:], in_=unit.rearrange("(p t) one -> p (t one)", t=PACK))
         w3_scale_rows = sb.tile([P, N], U8, name="w3_scale_rows", tag="w_scale_raw1", align_bytes=64)
         nc.gpsimd.memset(w3_scale_rows[:].bitcast(I32), 0)
-        load_scale_rows(nc.sync, w3_scale_rows, w3_scales, 1)
+        load_scale_rows(w3_scale_rows, w3_scales, 1, range(QUADS))
 
         def product(i, t):
             bank = psum.tile([P, S], F32, name="bank%d_%d" % (i, t), tag="bank%d" % (PACK * i + t))
@@ -132,57 +141,65 @@ def tile_picked_ysnowa_abs_p_kernel(
         ts = [product(0, t) for t in range(PACK)]
         ag = [product(1, t) for t in range(PACK)]
 
-        neg_ts = sb.tile([P, PACK * S + TS_SPARE], F32, name="neg_ts", tag="before_ln")
-        nc.vector.memset(neg_ts[:, PACK * S :], 0.0)
-        neg_ts_src = sb.tile([P, PACK, S], F32, name="neg_ts_src")
+        ts_rows = sb.tile([P, PACK * S + TS_SPARE], F32, name="ts_rows", tag="before_ln")
+        nc.vector.memset(ts_rows[:, PACK * S :], 0.0)
+        ts_src = sb.tile([P, PACK, S], F32, name="ts_src")
         melt = sb.tile([P, PACK, S], F32, name="melt")
         fresh = sb.tile([P, PACK, S], F32, name="fresh")
-        sig_src = sb.tile([P, PACK, S], F32, name="sig_src")
+        sig_src = sb.tile([P, PACK, S], F32, name="sig_src", tag="before_exp")
+        first = [(PACK - 1 - t) * S for t in range(PACK)]
+
+        def fetch_ts(t):
+            nc.vector.tensor_copy(ts_src[:, t, :], ts_rows[:, first[t] : first[t] + S + TS_SPARE].indirect(src_sb[:]))
+
+        nc.scalar.copy(ts_rows[:, first[0] : first[0] + S], ts[0][:])
+        for t in range(1, PACK):
+            nc.vector.tensor_copy(ts_rows[:, first[t] : first[t] + S], ts[t][:])
+            fetch_ts(t - 1)
+        fetch_ts(PACK - 1)
         for t in range(PACK):
-            lo = (PACK - 1 - t) * S
-            nc.vector.tensor_scalar(neg_ts[:, lo : lo + S], ts[t][:], -1.0, None, ALU.mult)
-            nc.vector.tensor_copy(neg_ts_src[:, t, :], neg_ts[:, lo : lo + S + TS_SPARE].indirect(src_sb[:]))
-        for t in range(PACK):
-            lo = (PACK - 1 - t) * S
-            nc.scalar.activation(melt[:, t, :], neg_ts[:, lo : lo + S], ACT.Sigmoid, scale=-2.0)
+            nc.scalar.activation(melt[:, t, :], ts_rows[:, first[t] : first[t] + S], ACT.Sigmoid, scale=2.0)
             nc.scalar.activation(fresh[:, t, :], ag[t][:], ACT.Sigmoid, scale=-1.0)
         for t in range(PACK):
-            nc.scalar.activation(sig_src[:, t, :], neg_ts_src[:, t, :], ACT.Sigmoid)
+            nc.scalar.activation(sig_src[:, t, :], ts_src[:, t, :], ACT.Sigmoid, scale=-1.0)
 
-        logs = sb.tile([P, 2, PACK, S], F32, name="logs", tag="before_ln")
-        ln_fresh = logs[:, 0]
-        ln_sig = logs[:, 1]
+        ln_fresh = sb.tile([P, PACK, S], F32, name="ln_fresh", tag="before_ln")
+        ln_sig = sb.tile([P, PACK, S], F32, name="ln_sig")
         dst = sb.tile([P, PACK, S], F32, name="dst")
-        ln_den = sb.tile([P, PACK, S], F32, name="ln_den")
         for t in range(PACK):
             nc.scalar.activation(ln_fresh[:, t, :], fresh[:, t, :], ACT.Ln, bias=TINY)
+        nc.scalar.activation(ln_sig[:], sig_src[:], ACT.Ln, bias=TINY)
+        age = [sb.tile([P, S + AGE_SPARE], F32, name="age%d" % t) for t in range(PACK)]
+
+        def fetch_age(t):
+            nc.vector.tensor_tensor(dst[:, t, :], age[t][:].indirect(src_sb[:]), dust_sb[:, t, :], ALU.mult)
+
         for t in range(PACK):
-            age = sb.tile([P, S + AGE_SPARE], F32, name="age%d" % t)
-            nc.vector.memset(age[:, S:], 0.0)
-            nc.vector.scalar_tensor_tensor(age[:, :S], ln_fresh[:, t, :], -1.0, ag[t][:], ALU.mult, ALU.max)
-            nc.vector.tensor_tensor(dst[:, t, :], age[:].indirect(src_sb[:]), dust_sb[:, t, :], ALU.mult)
-        for h in range(2):
-            nc.scalar.activation(ln_sig[:, 2 * h : 2 * h + 2, :], sig_src[:, 2 * h : 2 * h + 2, :], ACT.Ln, bias=TINY)
-        for t in range(PACK):
-            nc.scalar.activation(ln_den[:, t, :], dst[:, t, :], ACT.Ln, bias=1.0)
+            nc.vector.memset(age[t][:, S:], 0.0)
+            nc.vector.scalar_tensor_tensor(age[t][:, :S], ln_fresh[:, t, :], -1.0, ag[t][:], ALU.mult, ALU.max)
+            if t > 0:
+                fetch_age(t - 1)
+        fetch_age(PACK - 1)
+
+        halves = [slice(c, c + S // 2) for c in range(0, S, S // 2)]
+        chunks = [slice(c, c + CHUNK) for c in range(0, S, CHUNK)]
+        ratio = sb.tile([P, PACK, S], F32, name="ratio", tag="before_exp")
+        for cols in halves:
+            nc.scalar.activation(ratio[:, :, cols], ln_fresh[:, :, cols], ACT.Exp, scale=0.8)
+        root = sb.tile([P, PACK, S], F32, name="root", tag="before_ln")
+        inv_den = sb.tile([P, PACK, S], F32, name="inv_den")
+        for cols in halves:
+            nc.scalar.activation(root[:, :, cols], dst[:, :, cols], ACT.Abs_reciprocal_sqrt, bias=1.0)
+        for cols in halves:
+            nc.scalar.activation(inv_den[:, :, cols], root[:, :, cols], ACT.Square)
 
         neg_soft = sb.tile([P, PACK, S], F32, name="neg_soft")
         neg_gain = sb.tile([P, PACK, S], F32, name="neg_gain")
         for h in range(2):
             rows = slice(2 * h, 2 * h + 2)
-            nc.vector.tensor_tensor(neg_soft[:, rows, :], neg_ts_src[:, rows, :], ln_sig[:, rows, :], ALU.min)
+            nc.vector.scalar_tensor_tensor(neg_soft[:, rows, :], ts_src[:, rows, :], -1.0, ln_sig[:, rows, :], ALU.mult, ALU.min)
         for t in range(PACK):
-            nc.vector.tensor_scalar(neg_gain[:, t, :], neg_soft[:, t, :], unit_sb[:, t : t + 1], None, ALU.mult)
-
-        exps = sb.tile([P, 2, PACK, S], F32, name="exps", tag="x_word_rows0")
-        ratio = exps[:, 0]
-        inv_den = exps[:, 1]
-        halves = [slice(c, c + S // 2) for c in range(0, S, S // 2)]
-        chunks = [slice(c, c + CHUNK) for c in range(0, S, CHUNK)]
-        for cols in chunks:
-            nc.scalar.activation(ratio[:, :, cols], ln_fresh[:, :, cols], ACT.Exp, scale=0.8)
-        for cols in halves:
-            nc.scalar.activation(inv_den[:, :, cols], ln_den[:, :, cols], ACT.Exp, scale=-1.0)
+            nc.scalar.activation(neg_gain[:, t, :], neg_soft[:, t, :], ACT.Copy, scale=unit_sb[:, t : t + 1])
 
         mixed = sb.tile([P, PACK, S], F32, name="mixed")
         dark = sb.tile([P, PACK, S], F32, name="dark")
@@ -217,15 +234,14 @@ def tile_picked_ysnowa_abs_p_kernel(
             nc.scalar.copy(result[:], bands[:])
             nc.sync.dma_start(out=out[:, cols].rearrange("(m p) j -> p m j", p=P), in_=result[:])
 
-        for h in range(2):
-            pair = chunks[2 * h : 2 * h + 2]
-            for cols in pair:
-                nc.vector.scalar_tensor_tensor(mixed[:, :, cols], ratio[:, :, cols], -1.0, melt[:, :, cols], ALU.add, ALU.mult)
-            for cols in pair:
-                nc.vector.scalar_tensor_tensor(dark[:, :, cols], mixed[:, :, cols], 1.0, fresh[:, :, cols], ALU.add, ALU.mult)
-            for cols in pair:
-                nc.vector.scalar_tensor_tensor(alb[:, :, cols], dark[:, :, cols], 0.2, inv_den[:, :, cols], ALU.add, ALU.mult)
-            for cols in pair:
-                nc.vector.scalar_tensor_tensor(hid[:, :, cols], alb[:, :, cols], -1.0, neg_gain[:, :, cols], ALU.add, ALU.mult)
-            for c in range(2 * h, 2 * h + 2):
-                finish(c)
+        for cols in halves:
+            nc.vector.scalar_tensor_tensor(mixed[:, :, cols], ratio[:, :, cols], -1.0, melt[:, :, cols], ALU.add, ALU.mult)
+        for cols in halves:
+            nc.vector.scalar_tensor_tensor(dark[:, :, cols], mixed[:, :, cols], 1.0, fresh[:, :, cols], ALU.add, ALU.mult)
+        for cols in halves:
+            nc.vector.scalar_tensor_tensor(alb[:, :, cols], dark[:, :, cols], 0.2, inv_den[:, :, cols], ALU.add, ALU.mult)
+        for c, cols in enumerate(chunks):
+            nc.vector.scalar_tensor_tensor(hid[:, :, cols], alb[:, :, cols], -1.0, neg_gain[:, :, cols], ALU.add, ALU.mult)
+            if c > 0:
+                finish(c - 1)
+        finish(len(chunks) - 1)

@@ -40,10 +40,10 @@ def tile_picked_ysnowa_abs_p_kernel(
         nc.sync.dma_start(offs_sb[:], offs)
 
         def load_scale_rows(tile, rows, passes, quads):
-            for q in quads:
+            for r in quads:
                 nc.sync.dma_start(
-                    out=tile[32 * q : 32 * q + 4, :].bitcast(I32).rearrange("p (o c) -> p o c", o=passes),
-                    in_=rows[:, 4 * q : 4 * q + 4, :].bitcast(I32).rearrange("o r c -> r o c"),
+                    out=tile[r:P:32, :].bitcast(I32).rearrange("p (o c) -> p o c", o=passes),
+                    in_=rows[:, r:16:4, :].bitcast(I32).rearrange("o q c -> q o c"),
                 )
 
         x_scale_rows = sb.tile([P, PASSES * T], U8, name="x_scale_rows", tag="x_scale_rows", align_bytes=64)
@@ -152,13 +152,15 @@ def tile_picked_ysnowa_abs_p_kernel(
         def fetch_ts(t):
             nc.vector.tensor_copy(ts_src[:, t, :], ts_rows[:, first[t] : first[t] + S + TS_SPARE].indirect(src_sb[:]))
 
+        nc.scalar.activation(melt[:, 0, :], ts[0][:], ACT.Sigmoid, scale=2.0)
         nc.scalar.copy(ts_rows[:, first[0] : first[0] + S], ts[0][:])
         for t in range(1, PACK):
             nc.vector.tensor_copy(ts_rows[:, first[t] : first[t] + S], ts[t][:])
             fetch_ts(t - 1)
         fetch_ts(PACK - 1)
-        for t in range(PACK):
+        for t in range(1, PACK):
             nc.scalar.activation(melt[:, t, :], ts_rows[:, first[t] : first[t] + S], ACT.Sigmoid, scale=2.0)
+        for t in range(PACK):
             nc.scalar.activation(fresh[:, t, :], ag[t][:], ACT.Sigmoid, scale=-1.0)
         for t in range(PACK):
             nc.scalar.activation(sig_src[:, t, :], ts_src[:, t, :], ACT.Sigmoid, scale=-1.0)
@@ -186,12 +188,6 @@ def tile_picked_ysnowa_abs_p_kernel(
         ratio = sb.tile([P, PACK, S], F32, name="ratio", tag="before_exp")
         for cols in halves:
             nc.scalar.activation(ratio[:, :, cols], ln_fresh[:, :, cols], ACT.Exp, scale=0.8)
-        root = sb.tile([P, PACK, S], F32, name="root", tag="before_ln")
-        inv_den = sb.tile([P, PACK, S], F32, name="inv_den")
-        for cols in halves:
-            nc.scalar.activation(root[:, :, cols], dst[:, :, cols], ACT.Abs_reciprocal_sqrt, bias=1.0)
-        for cols in halves:
-            nc.scalar.activation(inv_den[:, :, cols], root[:, :, cols], ACT.Square)
 
         neg_soft = sb.tile([P, PACK, S], F32, name="neg_soft")
         neg_gain = sb.tile([P, PACK, S], F32, name="neg_gain")
@@ -200,6 +196,18 @@ def tile_picked_ysnowa_abs_p_kernel(
             nc.vector.scalar_tensor_tensor(neg_soft[:, rows, :], ts_src[:, rows, :], -1.0, ln_sig[:, rows, :], ALU.mult, ALU.min)
         for t in range(PACK):
             nc.scalar.activation(neg_gain[:, t, :], neg_soft[:, t, :], ACT.Copy, scale=unit_sb[:, t : t + 1])
+
+        root = sb.tile([P, PACK, S], F32, name="root", tag="before_ln")
+        inv_den = sb.tile([P, PACK, S], F32, name="inv_den")
+
+        def square(cols):
+            nc.scalar.activation(inv_den[:, :, cols], root[:, :, cols], ACT.Square)
+
+        for c, cols in enumerate(chunks):
+            nc.scalar.activation(root[:, :, cols], dst[:, :, cols], ACT.Abs_reciprocal_sqrt, bias=1.0)
+            if c > 0:
+                square(chunks[c - 1])
+        square(chunks[-1])
 
         mixed = sb.tile([P, PACK, S], F32, name="mixed")
         dark = sb.tile([P, PACK, S], F32, name="dark")
@@ -238,10 +246,16 @@ def tile_picked_ysnowa_abs_p_kernel(
             nc.vector.scalar_tensor_tensor(mixed[:, :, cols], ratio[:, :, cols], -1.0, melt[:, :, cols], ALU.add, ALU.mult)
         for cols in halves:
             nc.vector.scalar_tensor_tensor(dark[:, :, cols], mixed[:, :, cols], 1.0, fresh[:, :, cols], ALU.add, ALU.mult)
-        for cols in halves:
-            nc.vector.scalar_tensor_tensor(alb[:, :, cols], dark[:, :, cols], 0.2, inv_den[:, :, cols], ALU.add, ALU.mult)
-        for c, cols in enumerate(chunks):
+
+        def hidden(cols):
             nc.vector.scalar_tensor_tensor(hid[:, :, cols], alb[:, :, cols], -1.0, neg_gain[:, :, cols], ALU.add, ALU.mult)
+
+        for c, cols in enumerate(chunks):
+            nc.vector.scalar_tensor_tensor(alb[:, :, cols], dark[:, :, cols], 0.2, inv_den[:, :, cols], ALU.add, ALU.mult)
             if c > 0:
-                finish(c - 1)
+                hidden(chunks[c - 1])
+            if c > 1:
+                finish(c - 2)
+        hidden(chunks[-1])
+        finish(len(chunks) - 2)
         finish(len(chunks) - 1)

@@ -56,7 +56,7 @@ def tile_picked_ysnowa_abs_p_kernel(
             scale_raw = sb.tile([P, PASSES * H], U8, name="w_scale_raw%d" % i, tag="w_scale_raw%d" % i, align_bytes=64)
             nc.vector.memset(scale_raw[:].bitcast(I32), 0)
             w_scale_raw.append(scale_raw)
-        x_word_rows = [sb.tile([P, T], U32, name="x_word_rows%d" % o, tag="x_word_rows%d" % o) for o in range(PASSES)]
+        x_word_rows = [sb.tile([P, T], U32, name="x_word_rows%d" % o, tag="x_word_rows%d" % o, align_bytes=64) for o in range(PASSES)]
 
         def load_w_words(i, words):
             nc.sync.dma_start(
@@ -79,15 +79,19 @@ def tile_picked_ysnowa_abs_p_kernel(
         load_scale_rows(w_scale_raw[1], w2_scales, PASSES, range(QUADS))
         nc.sync.dma_start(src_sb[:], src)
 
-        def deal_words(i):
-            codes = sb.tile([P, PASSES * 2 * H], U8, name="w_codes%d" % i, align_bytes=64)
+        def deal_words(i, t0, t1, tag):
+            codes = sb.tile([P, PASSES * (t1 - t0) * 2 * P], U8, name="w_codes%d_%d" % (i, t0), tag=tag, align_bytes=64)
             nc.vector.tensor_copy(
-                out=codes[:].bitcast(U16).rearrange("p (o t g m) -> p o g t m", o=PASSES, t=PACK, m=8),
-                in_=w_raw[i][:].bitcast(U16).rearrange("p (o g m t) -> p o g t m", o=PASSES, t=PACK, m=8),
+                out=codes[:].bitcast(U16).rearrange("p (o t g m) -> p o g t m", o=PASSES, t=t1 - t0, m=8),
+                in_=w_raw[i][:].bitcast(U16).rearrange("p (o g m t) -> p o g t m", o=PASSES, t=PACK, m=8)[:, :, :, t0:t1, :],
             )
-            return codes
+            for t in range(t0, t1):
+                for o in range(PASSES):
+                    col = (o * (t1 - t0) + t - t0) * 2 * P
+                    w_codes[i, t, o] = codes[:, col : col + 2 * P]
 
-        w_codes = [deal_words(0)]
+        w_codes = {}
+        deal_words(0, 0, 2, "w1_codes_early")
         x_picked_scales = []
         for o in range(PASSES):
             picked = sb.tile([P, S], U8, name="x_picked_scales%d" % o, align_bytes=64)
@@ -110,10 +114,11 @@ def tile_picked_ysnowa_abs_p_kernel(
         x_codes = [pick_words(0, "x_codes0")]
         w_scales = [deal_scales(0, "x_scale_rows")]
         x_codes.append(pick_words(1, "w_scale_raw0"))
-        w_codes.append(deal_words(1))
+        deal_words(0, 2, PACK, "x_word_rows1")
+        deal_words(1, 0, PACK, "w2_codes")
         w_scales.append(deal_scales(1, "w_scales1"))
 
-        dust_sb = sb.tile([P, PACK, S], F32, name="dust_sb", tag="x_word_rows0")
+        dust_sb = sb.tile([P, PACK, S], F32, name="dust_sb", tag="x_word_rows0", align_bytes=64)
         nc.sync.dma_start(out=dust_sb[:], in_=dust.rearrange("(p t) j -> p t j", t=PACK))
         w3_codes = sb.tile([P, 2 * N], U8, name="w3_codes", tag="w_raw0", align_bytes=64)
         nc.sync.dma_start(out=w3_codes[:].bitcast(I32), in_=w3_words[0].bitcast(I32))
@@ -129,7 +134,7 @@ def tile_picked_ysnowa_abs_p_kernel(
                 col = (o * PACK + t) * P
                 nc.tensor.matmul_mx(
                     out=bank[:],
-                    lhsT=w_codes[i][:, 2 * col : 2 * (col + P)].bitcast(FP4X4),
+                    lhsT=w_codes[i, t, o].bitcast(FP4X4),
                     lhsT_scale=w_scales[i][:, col : col + P],
                     rhs=x_codes[o][:].bitcast(FP8X4),
                     rhs_scale=x_picked_scales[o][:],
@@ -141,49 +146,57 @@ def tile_picked_ysnowa_abs_p_kernel(
         ts = [product(0, t) for t in range(PACK)]
         ag = [product(1, t) for t in range(PACK)]
 
-        ts_rows = sb.tile([P, PACK * S + TS_SPARE], F32, name="ts_rows", tag="before_ln")
-        nc.vector.memset(ts_rows[:, PACK * S :], 0.0)
-        ts_src = sb.tile([P, PACK, S], F32, name="ts_src")
+        halves = [slice(c, c + S // 2) for c in range(0, S, S // 2)]
         melt = sb.tile([P, PACK, S], F32, name="melt")
         fresh = sb.tile([P, PACK, S], F32, name="fresh")
-        sig_src = sb.tile([P, PACK, S], F32, name="sig_src", tag="before_exp")
+        for t in range(PACK):
+            nc.scalar.activation(melt[:, t, :], ts[t][:], ACT.Sigmoid, scale=2.0)
+        for t in range(PACK):
+            nc.scalar.activation(fresh[:, t, :], ag[t][:], ACT.Sigmoid, scale=-1.0)
+
+        ts_rows = sb.tile([P, PACK * S + TS_SPARE], F32, name="ts_rows")
+        nc.vector.memset(ts_rows[:, PACK * S :], 0.0)
+        ts_src = sb.tile([P, PACK, S], F32, name="ts_src")
         first = [(PACK - 1 - t) * S for t in range(PACK)]
 
         def fetch_ts(t):
             nc.vector.tensor_copy(ts_src[:, t, :], ts_rows[:, first[t] : first[t] + S + TS_SPARE].indirect(src_sb[:]))
 
-        nc.scalar.activation(melt[:, 0, :], ts[0][:], ACT.Sigmoid, scale=2.0)
-        nc.scalar.copy(ts_rows[:, first[0] : first[0] + S], ts[0][:])
-        for t in range(1, PACK):
+        for t in range(PACK):
             nc.vector.tensor_copy(ts_rows[:, first[t] : first[t] + S], ts[t][:])
-            fetch_ts(t - 1)
+            if t > 0:
+                fetch_ts(t - 1)
         fetch_ts(PACK - 1)
-        for t in range(1, PACK):
-            nc.scalar.activation(melt[:, t, :], ts_rows[:, first[t] : first[t] + S], ACT.Sigmoid, scale=2.0)
-        for t in range(PACK):
-            nc.scalar.activation(fresh[:, t, :], ag[t][:], ACT.Sigmoid, scale=-1.0)
-        for t in range(PACK):
-            nc.scalar.activation(sig_src[:, t, :], ts_src[:, t, :], ACT.Sigmoid, scale=-1.0)
 
-        ln_fresh = sb.tile([P, PACK, S], F32, name="ln_fresh", tag="before_ln")
+        ln_fresh = sb.tile([P, PACK, S], F32, name="ln_fresh", tag="before_root")
+        tiny = sb.tile([P, 1], F32, name="tiny", tag="before_exp")
+        nc.vector.memset(tiny[:], TINY)
+        for cols in halves:
+            nc.scalar.activation(ln_fresh[:, :, cols], fresh[:, :, cols], ACT.Ln, bias=tiny[:])
+        sig_src = sb.tile([P, PACK, S], F32, name="sig_src", tag="before_exp")
+        nc.scalar.activation(sig_src[:], ts_src[:], ACT.Sigmoid, scale=-1.0)
         ln_sig = sb.tile([P, PACK, S], F32, name="ln_sig")
+        for h in range(2):
+            nc.scalar.activation(ln_sig[:, 2 * h : 2 * h + 2, :], sig_src[:, 2 * h : 2 * h + 2, :], ACT.Ln, bias=TINY)
+
         dst = sb.tile([P, PACK, S], F32, name="dst")
-        for t in range(PACK):
-            nc.scalar.activation(ln_fresh[:, t, :], fresh[:, t, :], ACT.Ln, bias=TINY)
-        nc.scalar.activation(ln_sig[:], sig_src[:], ACT.Ln, bias=TINY)
         age = [sb.tile([P, S + AGE_SPARE], F32, name="age%d" % t) for t in range(PACK)]
+
+        def make_age(t, cols):
+            nc.vector.scalar_tensor_tensor(age[t][:, cols], ln_fresh[:, t, cols], -1.0, ag[t][:, cols], ALU.mult, ALU.max)
 
         def fetch_age(t):
             nc.vector.tensor_tensor(dst[:, t, :], age[t][:].indirect(src_sb[:]), dust_sb[:, t, :], ALU.mult)
 
         for t in range(PACK):
             nc.vector.memset(age[t][:, S:], 0.0)
-            nc.vector.scalar_tensor_tensor(age[t][:, :S], ln_fresh[:, t, :], -1.0, ag[t][:], ALU.mult, ALU.max)
+            make_age(t, halves[0])
+        for t in range(PACK):
+            make_age(t, halves[1])
             if t > 0:
                 fetch_age(t - 1)
         fetch_age(PACK - 1)
 
-        halves = [slice(c, c + S // 2) for c in range(0, S, S // 2)]
         chunks = [slice(c, c + CHUNK) for c in range(0, S, CHUNK)]
         ratio = sb.tile([P, PACK, S], F32, name="ratio", tag="before_exp")
         for cols in halves:
@@ -195,9 +208,9 @@ def tile_picked_ysnowa_abs_p_kernel(
             rows = slice(2 * h, 2 * h + 2)
             nc.vector.scalar_tensor_tensor(neg_soft[:, rows, :], ts_src[:, rows, :], -1.0, ln_sig[:, rows, :], ALU.mult, ALU.min)
         for t in range(PACK):
-            nc.scalar.activation(neg_gain[:, t, :], neg_soft[:, t, :], ACT.Copy, scale=unit_sb[:, t : t + 1])
+            nc.vector.tensor_scalar(neg_gain[:, t, :], neg_soft[:, t, :], unit_sb[:, t : t + 1], None, ALU.mult)
 
-        root = sb.tile([P, PACK, S], F32, name="root", tag="before_ln")
+        root = sb.tile([P, PACK, S], F32, name="root", tag="before_root")
         inv_den = sb.tile([P, PACK, S], F32, name="inv_den")
 
         def square(cols):

@@ -199,7 +199,7 @@ def tile_picked_ysnowa_abs_p_kernel(
 
         chunks = [slice(c, c + CHUNK) for c in range(0, S, CHUNK)]
         ratio = sb.tile([P, PACK, S], F32, name="ratio", tag="before_exp")
-        for cols in halves:
+        for cols in chunks:
             nc.scalar.activation(ratio[:, :, cols], ln_fresh[:, :, cols], ACT.Exp, scale=0.8)
 
         neg_soft = sb.tile([P, PACK, S], F32, name="neg_soft")
@@ -218,9 +218,7 @@ def tile_picked_ysnowa_abs_p_kernel(
 
         for c, cols in enumerate(chunks):
             nc.scalar.activation(root[:, :, cols], dst[:, :, cols], ACT.Abs_reciprocal_sqrt, bias=1.0)
-            if c > 0:
-                square(chunks[c - 1])
-        square(chunks[-1])
+            square(cols)
 
         mixed = sb.tile([P, PACK, S], F32, name="mixed")
         dark = sb.tile([P, PACK, S], F32, name="dark")
@@ -240,10 +238,11 @@ def tile_picked_ysnowa_abs_p_kernel(
             nc.vector.quantize_mx(
                 out=hid_codes[:].bitcast(FP8X4), scales=hid_scales[:], in_=woven[:].rearrange("p j t -> p (j t)")
             )
-            bands = psum.tile([P, N // P, CHUNK], F32, name="bands%d" % c, tag="bank%d" % c)
+            result = sb.tile([P, N // P, CHUNK], F32, name="result%d" % c)
             for m in range(N // P):
+                bands = psum.tile([P, CHUNK], F32, name="bands%d_%d" % (c, m), tag="bank%d" % (2 * c + m))
                 nc.tensor.matmul_mx(
-                    out=bands[:, m, :],
+                    out=bands[:],
                     lhsT=w3_codes[:, 2 * m * P : 2 * (m + 1) * P].bitcast(FP4X4),
                     lhsT_scale=w3_scale_rows[:, m * P : (m + 1) * P],
                     rhs=hid_codes[:].bitcast(FP8X4),
@@ -251,14 +250,18 @@ def tile_picked_ysnowa_abs_p_kernel(
                     start=True,
                     stop=True,
                 )
-            result = sb.tile([P, N // P, CHUNK], F32, name="result%d" % c)
-            nc.scalar.copy(result[:], bands[:])
+                empty = nc.vector.tensor_copy if c == len(chunks) - 1 and m == 1 else nc.scalar.copy
+                empty(result[:, m, :], bands[:])
             nc.sync.dma_start(out=out[:, cols].rearrange("(m p) j -> p m j", p=P), in_=result[:])
 
-        for cols in halves:
-            nc.vector.scalar_tensor_tensor(mixed[:, :, cols], ratio[:, :, cols], -1.0, melt[:, :, cols], ALU.add, ALU.mult)
-        for cols in halves:
+        def darken(cols):
             nc.vector.scalar_tensor_tensor(dark[:, :, cols], mixed[:, :, cols], 1.0, fresh[:, :, cols], ALU.add, ALU.mult)
+
+        for c, cols in enumerate(chunks):
+            nc.vector.scalar_tensor_tensor(mixed[:, :, cols], ratio[:, :, cols], -1.0, melt[:, :, cols], ALU.add, ALU.mult)
+            if c > 0:
+                darken(chunks[c - 1])
+        darken(chunks[-1])
 
         def hidden(cols):
             nc.vector.scalar_tensor_tensor(hid[:, :, cols], alb[:, :, cols], -1.0, neg_gain[:, :, cols], ALU.add, ALU.mult)

from contextlib import ExitStack

import concourse.mybir as mybir

K, T, S, N, H = 1024, 2048, 512, 256, 512
FLOPS = 2 * (2 * K * H * S + H * N * S)

F32 = mybir.dt.float32
BF16 = mybir.dt.bfloat16
I32 = mybir.dt.int32
U32 = mybir.dt.uint32
U16 = mybir.dt.uint16
U8 = mybir.dt.uint8
FP8X4 = mybir.dt.float8_e4m3fn_x4
FP4X4 = mybir.dt.float4_e2m1fn_x4
ACT = mybir.ActivationFunctionType
ALU = mybir.AluOpType

P = 128
PACK = 4
PASSES = K // (P * PACK)
QUADS = 4
TS_SPARE = 192
AGE_SPARE = 32
CHUNK = 128
TINY = 2.0 ** -62


def tile_picked_ysnowa_abs_p_kernel(
    tc, x_words, x_scales, w1_words, w1_scales, w2_words, w2_scales, dust, unit, w3_words, w3_scales, offs, src, out
):
    nc = tc.nc
    with ExitStack() as ctx:
        lists = ctx.enter_context(tc.tile_pool(name="lists", bufs=1))
        sb = ctx.enter_context(tc.tile_pool(name="sb", bufs=1))
        psum = ctx.enter_context(tc.psum_pool(name="psum", bufs=1))

        offs_sb = lists.tile([P, S // 16], U16, name="offs_sb")
        src_sb = lists.tile([P, S // 16], U16, name="src_sb")
        nc.sync.dma_start(offs_sb[:], offs)

        def load_scale_rows(tile, rows, passes, quads):
            for r in quads:
                nc.sync.dma_start(
                    out=tile[r:P:32, :].bitcast(I32).rearrange("p (o c) -> p o c", o=passes),
                    in_=rows[:, r:16:4, :].bitcast(I32).rearrange("o q c -> q o c"),
                )

        x_scale_rows = sb.tile([P, PASSES * T], U8, name="x_scale_rows", tag="x_scale_rows", align_bytes=64)
        nc.vector.memset(x_scale_rows[:, :T].bitcast(I32), 0)
        nc.gpsimd.memset(x_scale_rows[:, T:].bitcast(I32), 0)
        w_raw = []
        w_scale_raw = []
        for i in range(2):
            w_raw.append(sb.tile([P, PASSES * 2 * H], U8, name="w_raw%d" % i, tag="w_raw%d" % i, align_bytes=64))
            scale_raw = sb.tile([P, PASSES * H], U8, name="w_scale_raw%d" % i, tag="w_scale_raw%d" % i, align_bytes=64)
            nc.vector.memset(scale_raw[:].bitcast(I32), 0)
            w_scale_raw.append(scale_raw)
        x_word_rows = [sb.tile([P, T], U32, name="x_word_rows%d" % o, tag="x_word_rows%d" % o, align_bytes=64) for o in range(PASSES)]

        def load_w_words(i, words):
            nc.sync.dma_start(
                out=w_raw[i][:].bitcast(I32).rearrange("p (o c) -> p o c", o=PASSES),
                in_=words.bitcast(I32).rearrange("o p c -> p o c"),
            )

        def load_x_words(o):
            nc.sync.dma_start(
                out=x_word_rows[o][:].bitcast(I32), in_=x_words[o].rearrange("p c r -> p (c r)").bitcast(I32)
            )

        load_w_words(0, w1_words)
        load_scale_rows(x_scale_rows, x_scales, PASSES, range(QUADS))
        load_scale_rows(w_scale_raw[0], w1_scales, PASSES, range(1))
        load_x_words(0)
        load_scale_rows(w_scale_raw[0], w1_scales, PASSES, range(1, QUADS))
        load_x_words(1)
        load_w_words(1, w2_words)
        load_scale_rows(w_scale_raw[1], w2_scales, PASSES, range(QUADS))
        nc.sync.dma_start(src_sb[:], src)

        def deal_words(i, t0, t1, tag):
            codes = sb.tile([P, PASSES * (t1 - t0) * 2 * P], U8, name="w_codes%d_%d" % (i, t0), tag=tag, align_bytes=64)
            nc.vector.tensor_copy(
                out=codes[:].bitcast(U16).rearrange("p (o t g m) -> p o g t m", o=PASSES, t=t1 - t0, m=8),
                in_=w_raw[i][:].bitcast(U16).rearrange("p (o g m t) -> p o g t m", o=PASSES, t=PACK, m=8)[:, :, :, t0:t1, :],
            )
            for t in range(t0, t1):
                for o in range(PASSES):
                    col = (o * (t1 - t0) + t - t0) * 2 * P
                    w_codes[i, t, o] = codes[:, col : col + 2 * P]

        w_codes = {}
        deal_words(0, 0, 2, "w1_codes_early")
        x_picked_scales = []
        for o in range(PASSES):
            picked = sb.tile([P, S], U8, name="x_picked_scales%d" % o, align_bytes=64)
            nc.vector.tensor_copy(picked[:], x_scale_rows[:, o * T : (o + 1) * T].indirect(offs_sb[:]))
            x_picked_scales.append(picked)

        def deal_scales(i, tag):
            scales = sb.tile([P, PASSES * H], U8, name="w_scales%d" % i, tag=tag, align_bytes=64)
            nc.vector.tensor_copy(
                out=scales[:].rearrange("p (o t g m) -> p o g t m", o=PASSES, t=PACK, m=16),
                in_=w_scale_raw[i][:].rearrange("p (o g m t) -> p o g t m", o=PASSES, t=PACK, m=16),
            )
            return scales

        def pick_words(o, tag):
            codes = sb.tile([P, S], U32, name="x_codes%d" % o, tag=tag, align_bytes=64)
            nc.vector.tensor_copy(codes[:], x_word_rows[o][:].indirect(offs_sb[:]))
            return codes

        x_codes = [pick_words(0, "x_codes0")]
        w_scales = [deal_scales(0, "x_scale_rows")]
        x_codes.append(pick_words(1, "w_scale_raw0"))
        deal_words(0, 2, PACK, "x_word_rows1")
        deal_words(1, 0, PACK, "w2_codes")
        w_scales.append(deal_scales(1, "w_scales1"))

        dust_sb = sb.tile([P, PACK, S], F32, name="dust_sb", tag="x_word_rows0", align_bytes=64)
        nc.sync.dma_start(out=dust_sb[:], in_=dust.rearrange("(p t) j -> p t j", t=PACK))
        w3_codes = sb.tile([P, 2 * N], U8, name="w3_codes", tag="w_raw0", align_bytes=64)
        nc.sync.dma_start(out=w3_codes[:].bitcast(I32), in_=w3_words[0].bitcast(I32))
        unit_sb = sb.tile([P, PACK], F32, name="unit_sb", tag="w_raw1", align_bytes=64)
        nc.sync.dma_start(out=unit_sb[:], in_=unit.rearrange("(p t) one -> p (t one)", t=PACK))
        w3_scale_rows = sb.tile([P, N], U8, name="w3_scale_rows", tag="w_scale_raw1", align_bytes=64)
        nc.gpsimd.memset(w3_scale_rows[:].bitcast(I32), 0)
        load_scale_rows(w3_scale_rows, w3_scales, 1, range(QUADS))

        def product(i, t):
            bank = psum.tile([P, S], F32, name="bank%d_%d" % (i, t), tag="bank%d" % (PACK * i + t))
            for o in range(PASSES):
                col = (o * PACK + t) * P
                nc.tensor.matmul_mx(
                    out=bank[:],
                    lhsT=w_codes[i, t, o].bitcast(FP4X4),
                    lhsT_scale=w_scales[i][:, col : col + P],
                    rhs=x_codes[o][:].bitcast(FP8X4),
                    rhs_scale=x_picked_scales[o][:],
                    start=(o == 0),
                    stop=(o == PASSES - 1),
                )
            return bank

        ts = [product(0, t) for t in range(PACK)]
        ag = [product(1, t) for t in range(PACK)]

        halves = [slice(c, c + S // 2) for c in range(0, S, S // 2)]
        melt = sb.tile([P, PACK, S], F32, name="melt")
        fresh = sb.tile([P, PACK, S], F32, name="fresh")
        for t in range(PACK):
            nc.scalar.activation(melt[:, t, :], ts[t][:], ACT.Sigmoid, scale=2.0)
        for t in range(PACK):
            nc.scalar.activation(fresh[:, t, :], ag[t][:], ACT.Sigmoid, scale=-1.0)

        ts_rows = sb.tile([P, PACK * S + TS_SPARE], F32, name="ts_rows")
        nc.vector.memset(ts_rows[:, PACK * S :], 0.0)
        ts_src = sb.tile([P, PACK, S], F32, name="ts_src")
        first = [(PACK - 1 - t) * S for t in range(PACK)]

        def fetch_ts(t):
            nc.vector.tensor_copy(ts_src[:, t, :], ts_rows[:, first[t] : first[t] + S + TS_SPARE].indirect(src_sb[:]))

        for t in range(PACK):
            nc.vector.tensor_copy(ts_rows[:, first[t] : first[t] + S], ts[t][:])
            if t > 0:
                fetch_ts(t - 1)
        fetch_ts(PACK - 1)

        ln_fresh = sb.tile([P, PACK, S], F32, name="ln_fresh", tag="before_root")
        tiny = sb.tile([P, 1], F32, name="tiny", tag="before_exp")
        nc.vector.memset(tiny[:], TINY)
        for cols in halves:
            nc.scalar.activation(ln_fresh[:, :, cols], fresh[:, :, cols], ACT.Ln, bias=tiny[:])
        sig_src = sb.tile([P, PACK, S], F32, name="sig_src", tag="before_exp")
        nc.scalar.activation(sig_src[:], ts_src[:], ACT.Sigmoid, scale=-1.0)
        ln_sig = sb.tile([P, PACK, S], F32, name="ln_sig")
        for h in range(2):
            nc.scalar.activation(ln_sig[:, 2 * h : 2 * h + 2, :], sig_src[:, 2 * h : 2 * h + 2, :], ACT.Ln, bias=TINY)

        dst = sb.tile([P, PACK, S], F32, name="dst")
        age = [sb.tile([P, S + AGE_SPARE], F32, name="age%d" % t) for t in range(PACK)]

        def make_age(t, cols):
            nc.vector.scalar_tensor_tensor(age[t][:, cols], ln_fresh[:, t, cols], -1.0, ag[t][:, cols], ALU.mult, ALU.max)

        def fetch_age(t):
            nc.vector.tensor_tensor(dst[:, t, :], age[t][:].indirect(src_sb[:]), dust_sb[:, t, :], ALU.mult)

        for t in range(PACK):
            nc.vector.memset(age[t][:, S:], 0.0)
            make_age(t, halves[0])
        for t in range(PACK):
            make_age(t, halves[1])
            if t > 0:
                fetch_age(t - 1)
        fetch_age(PACK - 1)

        chunks = [slice(c, c + CHUNK) for c in range(0, S, CHUNK)]
        ratio = sb.tile([P, PACK, S], F32, name="ratio", tag="before_exp")
        for cols in chunks:
            nc.scalar.activation(ratio[:, :, cols], ln_fresh[:, :, cols], ACT.Exp, scale=0.8)

        neg_soft = sb.tile([P, PACK, S], F32, name="neg_soft")
        neg_gain = sb.tile([P, PACK, S], F32, name="neg_gain")
        for h in range(2):
            rows = slice(2 * h, 2 * h + 2)
            nc.vector.scalar_tensor_tensor(neg_soft[:, rows, :], ts_src[:, rows, :], -1.0, ln_sig[:, rows, :], ALU.mult, ALU.min)
        for t in range(PACK):
            nc.vector.tensor_scalar(neg_gain[:, t, :], neg_soft[:, t, :], unit_sb[:, t : t + 1], None, ALU.mult)

        root = sb.tile([P, PACK, S], F32, name="root", tag="before_root")
        inv_den = sb.tile([P, PACK, S], F32, name="inv_den")

        def square(cols):
            nc.scalar.activation(inv_den[:, :, cols], root[:, :, cols], ACT.Square)

        for c, cols in enumerate(chunks):
            nc.scalar.activation(root[:, :, cols], dst[:, :, cols], ACT.Abs_reciprocal_sqrt, bias=1.0)
            square(cols)

        mixed = sb.tile([P, PACK, S], F32, name="mixed")
        dark = sb.tile([P, PACK, S], F32, name="dark")
        alb = sb.tile([P, PACK, S], F32, name="alb")
        hid = sb.tile([P, PACK, S], BF16, name="hid")

        def finish(c):
            cols = chunks[c]
            woven = sb.tile([P, CHUNK, PACK], BF16, name="woven%d" % c, align_bytes=64)
            weave = nc.vector.tensor_copy if c == len(chunks) - 1 else nc.scalar.copy
            weave(
                woven[:].rearrange("p (g i) t -> p g t i", i=4),
                hid[:, :, cols].rearrange("p t (g i) -> p g t i", i=4),
            )
            hid_codes = sb.tile([P, CHUNK], U32, name="hid_codes%d" % c, align_bytes=64)
            hid_scales = sb.tile([P, CHUNK], U8, name="hid_scales%d" % c, align_bytes=64)
            nc.vector.quantize_mx(
                out=hid_codes[:].bitcast(FP8X4), scales=hid_scales[:], in_=woven[:].rearrange("p j t -> p (j t)")
            )
            result = sb.tile([P, N // P, CHUNK], F32, name="result%d" % c)
            for m in range(N // P):
                bands = psum.tile([P, CHUNK], F32, name="bands%d_%d" % (c, m), tag="bank%d" % (2 * c + m))
                nc.tensor.matmul_mx(
                    out=bands[:],
                    lhsT=w3_codes[:, 2 * m * P : 2 * (m + 1) * P].bitcast(FP4X4),
                    lhsT_scale=w3_scale_rows[:, m * P : (m + 1) * P],
                    rhs=hid_codes[:].bitcast(FP8X4),
                    rhs_scale=hid_scales[:],
                    start=True,
                    stop=True,
                )
                empty = nc.vector.tensor_copy if c == len(chunks) - 1 and m == 1 else nc.scalar.copy
                empty(result[:, m, :], bands[:])
            nc.sync.dma_start(out=out[:, cols].rearrange("(m p) j -> p m j", p=P), in_=result[:])

        def darken(cols):
            nc.vector.scalar_tensor_tensor(dark[:, :, cols], mixed[:, :, cols], 1.0, fresh[:, :, cols], ALU.add, ALU.mult)

        for c, cols in enumerate(chunks):
            nc.vector.scalar_tensor_tensor(mixed[:, :, cols], ratio[:, :, cols], -1.0, melt[:, :, cols], ALU.add, ALU.mult)
            if c > 0:
                darken(chunks[c - 1])
        darken(chunks[-1])

        def hidden(cols):
            nc.vector.scalar_tensor_tensor(hid[:, :, cols], alb[:, :, cols], -1.0, neg_gain[:, :, cols], ALU.add, ALU.mult)

        for c, cols in enumerate(chunks):
            nc.vector.scalar_tensor_tensor(alb[:, :, cols], dark[:, :, cols], 0.2, inv_den[:, :, cols], ALU.add, ALU.mult)
            if c > 0:
                hidden(chunks[c - 1])
            if c > 1:
                finish(c - 2)
        hidden(chunks[-1])
        finish(len(chunks) - 2)
        finish(len(chunks) - 1)
